import numpy as np
import ml_dtypes


def mxq(x, axis, fmt="e4m3"):
    dtype, down = {"e4m3": (ml_dtypes.float8_e4m3fn, 7), "e5m2": (ml_dtypes.float8_e5m2, 14)}[fmt]
    v = np.moveaxis(np.asarray(x, np.float32).astype(ml_dtypes.bfloat16).astype(np.float64), axis, -1)
    blocks = v.reshape(v.shape[:-1] + (-1, 32))
    amax = np.abs(blocks).max(-1, keepdims=True)
    byte = np.maximum(np.where(amax > 0, np.frexp(amax)[1] - 1 + 127, 0) - down, 1)
    scale = np.exp2(byte - 127.0)
    codes = (blocks / scale).astype(np.float32).astype(dtype).astype(np.float64)
    return np.moveaxis((codes * scale).reshape(v.shape), -1, axis)


WIDE = False


def mx_kscale(k):
    if not WIDE:
        return np.ones(k)
    levels = np.array([10, -10, 5, -5, 0])
    if k % 512:
        return np.exp2(np.random.permutation(np.resize(levels, k // 32))).repeat(32)
    a = np.empty((k // 512, 16))
    for p in range(k // 512):
        a[p, :8] = np.random.permutation(np.resize(levels, 8))
        for g in range(8):
            far = levels[np.abs(levels - a[p, g]) >= 10]
            a[p, g + 8] = far[np.random.randint(len(far))]
    return np.exp2(a.ravel()).repeat(32)


def f64(x):
    return np.asarray(x).astype(np.float64)


def striped8(idx):
    return np.asarray(idx).reshape(8, -1, 16).transpose(0, 2, 1).reshape(128, -1).astype(np.uint16)


def unstriped8(offs):
    return offs.reshape(8, 16, -1).transpose(0, 2, 1).reshape(8, -1).astype(np.int64)


def pick8(x, idx, run):
    r = np.arange(len(x))
    return x[r[:, None], idx[r % (8 * run) // run]]


E2M1 = np.array([0.0, 0.5, 1.0, 1.5, 2.0, 3.0, 4.0, 6.0, -0.0, -0.5, -1.0, -1.5, -2.0, -3.0, -4.0, -6.0])


def pack_weight(w, fmt):
    k, n = w.shape
    w = f64(np.asarray(w, np.float32).astype(ml_dtypes.bfloat16)).reshape(k // 32, 32, n)
    amax = np.abs(w).max(1)
    if fmt == "e4m3":
        byte = np.frexp(amax)[1] - 1 + 127 - 7
    else:
        mant, ex = np.frexp(amax / 6.0)
        byte = np.where(mant > 0.5, ex, ex - 1) + 127
    byte = np.clip(np.where(amax > 0, byte, 1), 1, 254)
    scaled = (w * np.exp2(127.0 - byte)[:, None, :]).reshape(k, n).astype(np.float32)
    by_word = np.ascontiguousarray(scaled.reshape(k // 512, 128, 4, n).transpose(0, 1, 3, 2))
    if fmt == "e4m3":
        words = by_word.astype(ml_dtypes.float8_e4m3fn).view(np.uint8)
    else:
        c = by_word.astype(ml_dtypes.float4_e2m1fn).view(np.uint8) & 0xF
        words = (c[..., 0::2] | (c[..., 1::2] << 4)).reshape(k // 512, 128, 2 * n)
    return np.ascontiguousarray(words), np.ascontiguousarray(byte.astype(np.uint8).reshape(k // 512, 16, n))


def unpack_weight(words, scales, fmt):
    g, _, n = scales.shape
    words = np.ascontiguousarray(words).reshape(g, 128, n, -1)
    if fmt == "e4m3":
        vals = words.view(ml_dtypes.float8_e4m3fn).astype(np.float64)
    else:
        nib = np.empty((g, 128, n, 4), np.uint8)
        nib[..., 0::2] = words & 0xF
        nib[..., 1::2] = words >> 4
        vals = E2M1[nib]
    vals = vals * np.repeat(np.exp2(scales.astype(np.float64) - 127.0), 8, axis=1)[..., None]
    return vals.transpose(0, 1, 3, 2).reshape(g * 512, n)


def sigmoid(v):
    return 1.0 / (1.0 + np.exp(-v))


D, T, I, Q = 512, 1024, 512, 128


def setup_inputs():
    n = np.random.standard_normal
    idx = np.stack([np.random.permutation(T)[:I] for _ in range(8)])
    idx2 = np.stack([np.random.permutation(T)[:I] for _ in range(8)])
    idx3 = np.stack([np.random.permutation(T)[:I] for _ in range(8)])
    fd = mx_kscale(D)
    keysp = pack_weight(n((D, T)) / fd[:, None], "e4m3")
    return {
        "query": (n((D, Q)) * 1.5 / np.sqrt(D) * fd[:, None]).astype(np.float32),
        "keys_words": keysp[0],
        "keys_scales": keysp[1],
        "lam": (np.random.uniform(4.0, 9.0, (Q, 1))).astype(np.float32),
        "level": (np.random.uniform(0.05, 0.2, (Q, 1))).astype(np.float32),
        "base": (0.3 * n((Q, I))).astype(np.float32),
        "gain2": (np.random.uniform(0.5, 2.0, (Q, 1))).astype(np.float32),
        "offs": striped8(idx),
        "offs2": striped8(idx2),
        "offs3": striped8(idx3),
    }


def reference(query, keys_words, keys_scales, lam, level, base, gain2, offs, offs2, offs3):
    idx = unstriped8(offs)
    idx2 = unstriped8(offs2)
    idx3 = unstriped8(offs3)
    keysu = unpack_weight(keys_words, keys_scales, "e4m3")
    queryq = mxq(f64(query), 0, "e4m3")
    a = queryq.T @ keysu
    s = sigmoid(pick8(a, idx, 16)) * sigmoid(pick8(a, idx2, 16)) * sigmoid(pick8(a, idx3, 16)) * f64(lam)
    p = np.exp(s - np.max(s, axis=1, keepdims=True))
    r = p / np.sum(p, axis=1, keepdims=True)
    w = np.maximum(r - np.max(r, axis=1, keepdims=True) * f64(level), 0.0)
    y = np.tanh(w * f64(gain2) * 128.0) + f64(base)
    return y

@@ -1,0 +1,143 @@
+from contextlib import ExitStack
+
+import concourse.mybir as mybir
+
+F32 = mybir.dt.float32
+BF16 = mybir.dt.bfloat16
+I32 = mybir.dt.int32
+U32 = mybir.dt.uint32
+U16 = mybir.dt.uint16
+U8 = mybir.dt.uint8
+FP8X4 = mybir.dt.float8_e4m3fn_x4
+ACT = mybir.ActivationFunctionType
+ALU = mybir.AluOpType
+
+D, T, I, Q = 512, 1024, 512, 128
+P = 128
+PACK = 4
+FLOPS = 2 * D * T * Q
+
+N_MM = 256
+HALF = I // 2
+
+
+def tile_attend_chainproduct_excess_gated_heads_kernel(
+    tc, query, keys_words, keys_scales, lam, level, base, gain2, offs, offs2, offs3, out
+):
+    nc = tc.nc
+    with ExitStack() as ctx:
+        sb = ctx.enter_context(tc.tile_pool(name="sb", bufs=1))
+        psum = ctx.enter_context(tc.psum_pool(name="psum", bufs=1))
+
+        q_raw = sb.tile([P, PACK, Q], F32, name="q_raw")
+        nc.sync.dma_start(out=q_raw[:], in_=query.rearrange("(p j) w -> p j w", j=PACK))
+
+        lists = [sb.tile([P, I // 16], U16, name="list%d" % n) for n in range(3)]
+        nc.sync.dma_start(lists[0][:], offs)
+
+        k_scales = sb.tile([P, T], U8, name="k_scales", align_bytes=64)
+        nc.gpsimd.memset(k_scales[:].bitcast(I32), 0)
+        for quad in range(4):
+            nc.scalar.dma_start(
+                out=k_scales[32 * quad : 32 * quad + 4, :].bitcast(I32),
+                in_=keys_scales[0, 4 * quad : 4 * quad + 4, :].bitcast(I32),
+            )
+
+        words = keys_words[0].rearrange("p n t -> p (n t)").bitcast(I32)
+        k_words = []
+        for h in range(2):
+            kw = sb.tile([P, T // 2], U32, name="k_words%d" % h, align_bytes=64)
+            nc.sync.dma_start(out=kw[:].bitcast(I32), in_=words[:, h * (T // 2) : (h + 1) * (T // 2)])
+            k_words.append(kw)
+
+        lam_t = sb.tile([P, 1], F32, name="lam_t")
+        gain_t = sb.tile([P, 1], F32, name="gain_t")
+        level_t = sb.tile([P, 1], F32, name="level_t")
+
+        nc.sync.dma_start(lists[1][:], offs2)
+        nc.sync.dma_start(lists[2][:], offs3)
+
+        nc.sync.dma_start(out=lam_t[:], in_=lam)
+        nc.sync.dma_start(out=gain_t[:], in_=gain2)
+        nc.sync.dma_start(out=level_t[:], in_=level)
+        base_t = sb.tile([P, I], F32, name="base_t")
+        nc.sync.dma_start(out=base_t[:], in_=base)
+
+        neg_lam8 = sb.tile([P, 1], F32, name="neg_lam8")
+        nc.gpsimd.tensor_scalar(neg_lam8[:], lam_t[:], -1.0, 0.0, ALU.mult, ALU.add)
+        gain128 = sb.tile([P, 1], F32, name="gain128")
+        nc.gpsimd.tensor_scalar(gain128[:], gain_t[:], 128.0, 0.0, ALU.mult, ALU.add)
+
+        q_bf = sb.tile([P, Q, PACK], BF16, name="q_bf", align_bytes=64)
+        nc.vector.tensor_copy(
+            out=q_bf[:].rearrange("p (c i) t -> p c t i", i=4),
+            in_=q_raw[:].rearrange("p t (c i) -> p c t i", i=4),
+        )
+        q_words = sb.tile([P, Q], U32, name="q_words", align_bytes=64)
+        q_scales = sb.tile([P, Q], U8, name="q_scales", align_bytes=64)
+        nc.vector.quantize_mx(
+            out=q_words[:].bitcast(FP8X4), scales=q_scales[:], in_=q_bf[:].rearrange("p w t -> p (w t)")
+        )
+
+        a = sb.tile([P, T], F32, name="a")
+        for n in range(T // N_MM):
+            bank = psum.tile([P, N_MM], F32, name="bank%d" % n)
+            h, c0 = divmod(n * N_MM, T // 2)
+            nc.tensor.matmul_mx(
+                out=bank[:],
+                lhsT=q_words[:].bitcast(FP8X4),
+                lhsT_scale=q_scales[:],
+                rhs=k_words[h][:, c0 : c0 + N_MM].bitcast(FP8X4),
+                rhs_scale=k_scales[:, n * N_MM : (n + 1) * N_MM],
+                start=True,
+                stop=True,
+            )
+            cols = slice(n * N_MM, (n + 1) * N_MM)
+            nc.vector.tensor_copy(a[:, cols], bank[:])
+
+        g = [sb.tile([P, I], F32, name="g%d" % n) for n in range(2)]
+        sig = [sb.tile([P, I], F32, name="sig%d" % n) for n in range(3)]
+        y = sb.tile([P, I], F32, name="y")
+        z = sb.tile([P, I], F32, name="z")
+        u = sb.tile([P, I], F32, name="u")
+        low = [sb.tile([P, 1], F32, name="low%d" % h) for h in range(2)]
+        halves = [slice(h * HALF, (h + 1) * HALF) for h in range(2)]
+
+        nc.scalar.activation(sig[0][:], a[:].indirect(lists[0][:]), ACT.Sigmoid)
+        nc.vector.tensor_copy(g[0][:], a[:].indirect(lists[1][:]))
+        for h in range(2):
+            part = lists[2][:, h * (HALF // 16) : (h + 1) * (HALF // 16)]
+            nc.vector.tensor_copy(g[1][:, halves[h]], a[:].indirect(part))
+        nc.scalar.activation(sig[1][:], g[0][:], ACT.Sigmoid)
+        for h in range(2):
+            nc.scalar.activation(sig[2][:, halves[h]], g[1][:, halves[h]], ACT.Sigmoid)
+        nc.vector.tensor_tensor(y[:], sig[0][:], sig[1][:], ALU.mult)
+        for h in range(2):
+            nc.vector.tensor_tensor(z[:, halves[h]], y[:, halves[h]], sig[2][:, halves[h]], ALU.mult)
+        for h in range(2):
+            start = None if h == 0 else low[0][:]
+            nc.vector.tensor_scalar(
+                u[:, halves[h]], z[:, halves[h]], neg_lam8[:], start, ALU.mult, ALU.min, accum_out=low[h][:]
+            )
+
+        p = sb.tile([P, I], F32, name="p")
+        total = sb.tile([P, 1], F32, name="total")
+        nc.scalar.activation(p[:], u[:], ACT.Exp, bias=low[1][:], scale=-1.0, accum_out=total[:])
+        inv = sb.tile([P, 1], F32, name="inv")
+        factor = sb.tile([P, 1], F32, name="factor")
+        ex = [sb.tile([P, HALF], F32, name="ex%d" % h) for h in range(2)]
+        th = [sb.tile([P, HALF], F32, name="th%d" % h) for h in range(2)]
+        res = [sb.tile([P, HALF], F32, name="res%d" % h) for h in range(2)]
+
+        def excess(h):
+            nc.vector.tensor_scalar(ex[h][:], p[:, h * HALF : (h + 1) * HALF], level_t[:], 0.0, ALU.subtract, ALU.max)
+
+        nc.vector.reciprocal(inv[:], total[:])
+        excess(0)
+        nc.vector.tensor_scalar(factor[:], inv[:], gain128[:], None, ALU.mult)
+        excess(1)
+        for h in range(2):
+            cols = slice(h * HALF, (h + 1) * HALF)
+            nc.scalar.activation(th[h][:], ex[h][:], ACT.Tanh, scale=factor[:])
+            nc.vector.tensor_tensor(res[h][:], th[h][:], base_t[:, cols], ALU.add)
+            nc.sync.dma_start(out=out[:, cols], in_=res[h][:])

@@ -35,20 +35,17 @@ def tile_attend_chainproduct_excess_gated_heads_kernel(
         lists = [sb.tile([P, I // 16], U16, name="list%d" % n) for n in range(3)]
         nc.sync.dma_start(lists[0][:], offs)
 
+        words = keys_words[0].rearrange("p n t -> p (n t)").bitcast(I32)
+        k_words = [sb.tile([P, T // 2], U32, name="k_words%d" % h, align_bytes=64) for h in range(2)]
         k_scales = sb.tile([P, T], U8, name="k_scales", align_bytes=64)
         nc.gpsimd.memset(k_scales[:].bitcast(I32), 0)
+        nc.sync.dma_start(out=k_words[0][:].bitcast(I32), in_=words[:, : T // 2])
         for quad in range(4):
-            nc.scalar.dma_start(
+            nc.sync.dma_start(
                 out=k_scales[32 * quad : 32 * quad + 4, :].bitcast(I32),
                 in_=keys_scales[0, 4 * quad : 4 * quad + 4, :].bitcast(I32),
             )
-
-        words = keys_words[0].rearrange("p n t -> p (n t)").bitcast(I32)
-        k_words = []
-        for h in range(2):
-            kw = sb.tile([P, T // 2], U32, name="k_words%d" % h, align_bytes=64)
-            nc.sync.dma_start(out=kw[:].bitcast(I32), in_=words[:, h * (T // 2) : (h + 1) * (T // 2)])
-            k_words.append(kw)
+        nc.sync.dma_start(out=k_words[1][:].bitcast(I32), in_=words[:, T // 2 :])
 
         lam_t = sb.tile([P, 1], F32, name="lam_t")
         gain_t = sb.tile([P, 1], F32, name="gain_t")
@@ -68,16 +65,21 @@ def tile_attend_chainproduct_excess_gated_heads_kernel(
         gain128 = sb.tile([P, 1], F32, name="gain128")
         nc.gpsimd.tensor_scalar(gain128[:], gain_t[:], 128.0, 0.0, ALU.mult, ALU.add)
 
-        q_bf = sb.tile([P, Q, PACK], BF16, name="q_bf", align_bytes=64)
-        nc.vector.tensor_copy(
-            out=q_bf[:].rearrange("p (c i) t -> p c t i", i=4),
-            in_=q_raw[:].rearrange("p t (c i) -> p c t i", i=4),
-        )
+        q_bf = [sb.tile([P, Q // 2, PACK], BF16, name="q_bf%d" % h, align_bytes=64) for h in range(2)]
         q_words = sb.tile([P, Q], U32, name="q_words", align_bytes=64)
         q_scales = sb.tile([P, Q], U8, name="q_scales", align_bytes=64)
-        nc.vector.quantize_mx(
-            out=q_words[:].bitcast(FP8X4), scales=q_scales[:], in_=q_bf[:].rearrange("p w t -> p (w t)")
-        )
+        q_cols = [slice(h * (Q // 2), (h + 1) * (Q // 2)) for h in range(2)]
+        for h in range(2):
+            nc.vector.tensor_copy(
+                out=q_bf[h][:].rearrange("p (c i) t -> p c t i", i=4),
+                in_=q_raw[:, :, q_cols[h]].rearrange("p t (c i) -> p c t i", i=4),
+            )
+        for h in range(2):
+            nc.vector.quantize_mx(
+                out=q_words[:, q_cols[h]].bitcast(FP8X4),
+                scales=q_scales[:, q_cols[h]],
+                in_=q_bf[h][:].rearrange("p w t -> p (w t)"),
+            )
 
         a = sb.tile([P, T], F32, name="a")
         for n in range(T // N_MM):
@@ -125,19 +127,19 @@ def tile_attend_chainproduct_excess_gated_heads_kernel(
         nc.scalar.activation(p[:], u[:], ACT.Exp, bias=low[1][:], scale=-1.0, accum_out=total[:])
         inv = sb.tile([P, 1], F32, name="inv")
         factor = sb.tile([P, 1], F32, name="factor")
-        ex = [sb.tile([P, HALF], F32, name="ex%d" % h) for h in range(2)]
-        th = [sb.tile([P, HALF], F32, name="th%d" % h) for h in range(2)]
-        res = [sb.tile([P, HALF], F32, name="res%d" % h) for h in range(2)]
+        parts = [slice(0, 256), slice(256, 384), slice(384, 512)]
+        ex = sb.tile([P, I], F32, name="ex")
+        th = sb.tile([P, I], F32, name="th")
+        res = sb.tile([P, I], F32, name="res")
 
         def excess(h):
-            nc.vector.tensor_scalar(ex[h][:], p[:, h * HALF : (h + 1) * HALF], level_t[:], 0.0, ALU.subtract, ALU.max)
+            nc.vector.tensor_scalar(ex[:, halves[h]], p[:, halves[h]], level_t[:], 0.0, ALU.subtract, ALU.max)
 
         nc.vector.reciprocal(inv[:], total[:])
         excess(0)
         nc.vector.tensor_scalar(factor[:], inv[:], gain128[:], None, ALU.mult)
         excess(1)
-        for h in range(2):
-            cols = slice(h * HALF, (h + 1) * HALF)
-            nc.scalar.activation(th[h][:], ex[h][:], ACT.Tanh, scale=factor[:])
-            nc.vector.tensor_tensor(res[h][:], th[h][:], base_t[:, cols], ALU.add)
-            nc.sync.dma_start(out=out[:, cols], in_=res[h][:])
+        for cols, queue in zip(parts, (nc.sync, nc.sync, nc.scalar)):
+            nc.scalar.activation(th[:, cols], ex[:, cols], ACT.Tanh, scale=factor[:])
+            nc.vector.tensor_tensor(res[:, cols], th[:, cols], base_t[:, cols], ALU.add)
+            queue.dma_start(out=out[:, cols], in_=res[:, cols])

@@ -38,7 +38,7 @@ def tile_attend_chainproduct_excess_gated_heads_kernel(
         words = keys_words[0].rearrange("p n t -> p (n t)").bitcast(I32)
         k_words = [sb.tile([P, T // 2], U32, name="k_words%d" % h, align_bytes=64) for h in range(2)]
         k_scales = sb.tile([P, T], U8, name="k_scales", align_bytes=64)
-        nc.gpsimd.memset(k_scales[:].bitcast(I32), 0)
+        nc.vector.memset(k_scales[:].bitcast(I32), 0)
         nc.sync.dma_start(out=k_words[0][:].bitcast(I32), in_=words[:, : T // 2])
         for quad in range(4):
             nc.sync.dma_start(
@@ -51,19 +51,14 @@ def tile_attend_chainproduct_excess_gated_heads_kernel(
         gain_t = sb.tile([P, 1], F32, name="gain_t")
         level_t = sb.tile([P, 1], F32, name="level_t")
 
-        nc.sync.dma_start(lists[1][:], offs2)
         nc.sync.dma_start(lists[2][:], offs3)
+        nc.sync.dma_start(lists[1][:], offs2)
 
         nc.sync.dma_start(out=lam_t[:], in_=lam)
         nc.sync.dma_start(out=gain_t[:], in_=gain2)
         nc.sync.dma_start(out=level_t[:], in_=level)
         base_t = sb.tile([P, I], F32, name="base_t")
         nc.sync.dma_start(out=base_t[:], in_=base)
-
-        neg_lam8 = sb.tile([P, 1], F32, name="neg_lam8")
-        nc.gpsimd.tensor_scalar(neg_lam8[:], lam_t[:], -1.0, 0.0, ALU.mult, ALU.add)
-        gain128 = sb.tile([P, 1], F32, name="gain128")
-        nc.gpsimd.tensor_scalar(gain128[:], gain_t[:], 128.0, 0.0, ALU.mult, ALU.add)
 
         q_bf = [sb.tile([P, Q // 2, PACK], BF16, name="q_bf%d" % h, align_bytes=64) for h in range(2)]
         q_words = sb.tile([P, Q], U32, name="q_words", align_bytes=64)
@@ -97,49 +92,49 @@ def tile_attend_chainproduct_excess_gated_heads_kernel(
             cols = slice(n * N_MM, (n + 1) * N_MM)
             nc.vector.tensor_copy(a[:, cols], bank[:])
 
-        g = [sb.tile([P, I], F32, name="g%d" % n) for n in range(2)]
+        g1 = sb.tile([P, HALF], F32, name="g1")
+        g2 = sb.tile([P, I], F32, name="g2")
         sig = [sb.tile([P, I], F32, name="sig%d" % n) for n in range(3)]
         y = sb.tile([P, I], F32, name="y")
         z = sb.tile([P, I], F32, name="z")
-        u = sb.tile([P, I], F32, name="u")
-        low = [sb.tile([P, 1], F32, name="low%d" % h) for h in range(2)]
+        low = sb.tile([P, 1], F32, name="low")
         halves = [slice(h * HALF, (h + 1) * HALF) for h in range(2)]
+        list_halves = [slice(h * HALF // 16, (h + 1) * HALF // 16) for h in range(2)]
 
         nc.scalar.activation(sig[0][:], a[:].indirect(lists[0][:]), ACT.Sigmoid)
-        nc.vector.tensor_copy(g[0][:], a[:].indirect(lists[1][:]))
-        for h in range(2):
-            part = lists[2][:, h * (HALF // 16) : (h + 1) * (HALF // 16)]
-            nc.vector.tensor_copy(g[1][:, halves[h]], a[:].indirect(part))
-        nc.scalar.activation(sig[1][:], g[0][:], ACT.Sigmoid)
-        for h in range(2):
-            nc.scalar.activation(sig[2][:, halves[h]], g[1][:, halves[h]], ACT.Sigmoid)
-        nc.vector.tensor_tensor(y[:], sig[0][:], sig[1][:], ALU.mult)
-        for h in range(2):
-            nc.vector.tensor_tensor(z[:, halves[h]], y[:, halves[h]], sig[2][:, halves[h]], ALU.mult)
-        for h in range(2):
-            start = None if h == 0 else low[0][:]
-            nc.vector.tensor_scalar(
-                u[:, halves[h]], z[:, halves[h]], neg_lam8[:], start, ALU.mult, ALU.min, accum_out=low[h][:]
+        nc.scalar.activation(sig[1][:, halves[0]], a[:].indirect(lists[1][:, list_halves[0]]), ACT.Sigmoid)
+        nc.vector.tensor_copy(g2[:], a[:].indirect(lists[2][:]))
+        nc.vector.tensor_copy(g1[:], a[:].indirect(lists[1][:, list_halves[1]]))
+        nc.scalar.activation(sig[2][:], g2[:], ACT.Sigmoid)
+        nc.scalar.activation(sig[1][:, halves[1]], g1[:], ACT.Sigmoid)
+        for h, (early, late) in enumerate(((1, 2), (2, 1))):
+            nc.vector.scalar_tensor_tensor(
+                y[:, halves[h]], sig[0][:, halves[h]], lam_t[:], sig[early][:, halves[h]], ALU.mult, ALU.mult
             )
+        for h, (early, late) in enumerate(((1, 2), (2, 1))):
+            nc.vector.tensor_tensor(z[:, halves[h]], y[:, halves[h]], sig[late][:, halves[h]], ALU.mult)
+        nc.vector.tensor_reduce(low[:], z[:], mybir.AxisListType.X, ALU.max, negate=True)
 
         p = sb.tile([P, I], F32, name="p")
         total = sb.tile([P, 1], F32, name="total")
-        nc.scalar.activation(p[:], u[:], ACT.Exp, bias=low[1][:], scale=-1.0, accum_out=total[:])
+        nc.scalar.activation(p[:], z[:], ACT.Exp, bias=low[:], accum_out=total[:])
         inv = sb.tile([P, 1], F32, name="inv")
         factor = sb.tile([P, 1], F32, name="factor")
-        parts = [slice(0, 256), slice(256, 384), slice(384, 512)]
         ex = sb.tile([P, I], F32, name="ex")
         th = sb.tile([P, I], F32, name="th")
         res = sb.tile([P, I], F32, name="res")
 
-        def excess(h):
-            nc.vector.tensor_scalar(ex[:, halves[h]], p[:, halves[h]], level_t[:], 0.0, ALU.subtract, ALU.max)
-
         nc.vector.reciprocal(inv[:], total[:])
-        excess(0)
-        nc.vector.tensor_scalar(factor[:], inv[:], gain128[:], None, ALU.mult)
-        excess(1)
-        for cols, queue in zip(parts, (nc.sync, nc.sync, nc.scalar)):
+        nc.vector.tensor_scalar(ex[:], p[:], level_t[:], 0.0, ALU.subtract, ALU.max)
+        nc.vector.tensor_scalar(factor[:], inv[:], gain_t[:], 128.0, ALU.mult, ALU.mult)
+        quarter = I // 4
+        for n in range(4):
+            cols = slice(n * quarter, (n + 1) * quarter)
             nc.scalar.activation(th[:, cols], ex[:, cols], ACT.Tanh, scale=factor[:])
             nc.vector.tensor_tensor(res[:, cols], th[:, cols], base_t[:, cols], ALU.add)
+        for cols, queue in (
+            (slice(0, 2 * quarter), nc.sync),
+            (slice(2 * quarter, 3 * quarter), nc.sync),
+            (slice(3 * quarter, I), nc.scalar),
+        ):
             queue.dma_start(out=out[:, cols], in_=res[:, cols])

@@ -105,7 +105,8 @@ def tile_attend_chainproduct_excess_gated_heads_kernel(
         nc.scalar.activation(sig[1][:, halves[0]], a[:].indirect(lists[1][:, list_halves[0]]), ACT.Sigmoid)
         nc.vector.tensor_copy(g2[:], a[:].indirect(lists[2][:]))
         nc.vector.tensor_copy(g1[:], a[:].indirect(lists[1][:, list_halves[1]]))
-        nc.scalar.activation(sig[2][:], g2[:], ACT.Sigmoid)
+        for h in (1, 0):
+            nc.scalar.activation(sig[2][:, halves[h]], g2[:, halves[h]], ACT.Sigmoid)
         nc.scalar.activation(sig[1][:, halves[1]], g1[:], ACT.Sigmoid)
         for h, (early, late) in enumerate(((1, 2), (2, 1))):
             nc.vector.scalar_tensor_tensor(

from contextlib import ExitStack

import concourse.mybir as mybir

F32 = mybir.dt.float32
BF16 = mybir.dt.bfloat16
I32 = mybir.dt.int32
U32 = mybir.dt.uint32
U16 = mybir.dt.uint16
U8 = mybir.dt.uint8
FP8X4 = mybir.dt.float8_e4m3fn_x4
ACT = mybir.ActivationFunctionType
ALU = mybir.AluOpType

D, T, I, Q = 512, 1024, 512, 128
P = 128
PACK = 4
FLOPS = 2 * D * T * Q

N_MM = 256
HALF = I // 2


def tile_attend_chainproduct_excess_gated_heads_kernel(
    tc, query, keys_words, keys_scales, lam, level, base, gain2, offs, offs2, offs3, out
):
    nc = tc.nc
    with ExitStack() as ctx:
        sb = ctx.enter_context(tc.tile_pool(name="sb", bufs=1))
        psum = ctx.enter_context(tc.psum_pool(name="psum", bufs=1))

        q_raw = sb.tile([P, PACK, Q], F32, name="q_raw")
        nc.sync.dma_start(out=q_raw[:], in_=query.rearrange("(p j) w -> p j w", j=PACK))

        lists = [sb.tile([P, I // 16], U16, name="list%d" % n) for n in range(3)]
        nc.sync.dma_start(lists[0][:], offs)

        words = keys_words[0].rearrange("p n t -> p (n t)").bitcast(I32)
        k_words = [sb.tile([P, T // 2], U32, name="k_words%d" % h, align_bytes=64) for h in range(2)]
        k_scales = sb.tile([P, T], U8, name="k_scales", align_bytes=64)
        nc.vector.memset(k_scales[:].bitcast(I32), 0)
        nc.sync.dma_start(out=k_words[0][:].bitcast(I32), in_=words[:, : T // 2])
        for quad in range(4):
            nc.sync.dma_start(
                out=k_scales[32 * quad : 32 * quad + 4, :].bitcast(I32),
                in_=keys_scales[0, 4 * quad : 4 * quad + 4, :].bitcast(I32),
            )
        nc.sync.dma_start(out=k_words[1][:].bitcast(I32), in_=words[:, T // 2 :])

        lam_t = sb.tile([P, 1], F32, name="lam_t")
        gain_t = sb.tile([P, 1], F32, name="gain_t")
        level_t = sb.tile([P, 1], F32, name="level_t")

        nc.sync.dma_start(lists[2][:], offs3)
        nc.sync.dma_start(lists[1][:], offs2)

        nc.sync.dma_start(out=lam_t[:], in_=lam)
        nc.sync.dma_start(out=gain_t[:], in_=gain2)
        nc.sync.dma_start(out=level_t[:], in_=level)
        base_t = sb.tile([P, I], F32, name="base_t")
        nc.sync.dma_start(out=base_t[:], in_=base)

        q_bf = [sb.tile([P, Q // 2, PACK], BF16, name="q_bf%d" % h, align_bytes=64) for h in range(2)]
        q_words = sb.tile([P, Q], U32, name="q_words", align_bytes=64)
        q_scales = sb.tile([P, Q], U8, name="q_scales", align_bytes=64)
        q_cols = [slice(h * (Q // 2), (h + 1) * (Q // 2)) for h in range(2)]
        for h in range(2):
            nc.vector.tensor_copy(
                out=q_bf[h][:].rearrange("p (c i) t -> p c t i", i=4),
                in_=q_raw[:, :, q_cols[h]].rearrange("p t (c i) -> p c t i", i=4),
            )
        for h in range(2):
            nc.vector.quantize_mx(
                out=q_words[:, q_cols[h]].bitcast(FP8X4),
                scales=q_scales[:, q_cols[h]],
                in_=q_bf[h][:].rearrange("p w t -> p (w t)"),
            )

        a = sb.tile([P, T], F32, name="a")
        for n in range(T // N_MM):
            bank = psum.tile([P, N_MM], F32, name="bank%d" % n)
            h, c0 = divmod(n * N_MM, T // 2)
            nc.tensor.matmul_mx(
                out=bank[:],
                lhsT=q_words[:].bitcast(FP8X4),
                lhsT_scale=q_scales[:],
                rhs=k_words[h][:, c0 : c0 + N_MM].bitcast(FP8X4),
                rhs_scale=k_scales[:, n * N_MM : (n + 1) * N_MM],
                start=True,
                stop=True,
            )
            cols = slice(n * N_MM, (n + 1) * N_MM)
            nc.vector.tensor_copy(a[:, cols], bank[:])

        g1 = sb.tile([P, HALF], F32, name="g1")
        g2 = sb.tile([P, I], F32, name="g2")
        sig = [sb.tile([P, I], F32, name="sig%d" % n) for n in range(3)]
        y = sb.tile([P, I], F32, name="y")
        z = sb.tile([P, I], F32, name="z")
        low = sb.tile([P, 1], F32, name="low")
        halves = [slice(h * HALF, (h + 1) * HALF) for h in range(2)]
        list_halves = [slice(h * HALF // 16, (h + 1) * HALF // 16) for h in range(2)]

        nc.scalar.activation(sig[0][:], a[:].indirect(lists[0][:]), ACT.Sigmoid)
        nc.scalar.activation(sig[1][:, halves[0]], a[:].indirect(lists[1][:, list_halves[0]]), ACT.Sigmoid)
        nc.vector.tensor_copy(g2[:], a[:].indirect(lists[2][:]))
        nc.vector.tensor_copy(g1[:], a[:].indirect(lists[1][:, list_halves[1]]))
        for h in (1, 0):
            nc.scalar.activation(sig[2][:, halves[h]], g2[:, halves[h]], ACT.Sigmoid)
        nc.scalar.activation(sig[1][:, halves[1]], g1[:], ACT.Sigmoid)
        for h, (early, late) in enumerate(((1, 2), (2, 1))):
            nc.vector.scalar_tensor_tensor(
                y[:, halves[h]], sig[0][:, halves[h]], lam_t[:], sig[early][:, halves[h]], ALU.mult, ALU.mult
            )
        for h, (early, late) in enumerate(((1, 2), (2, 1))):
            nc.vector.tensor_tensor(z[:, halves[h]], y[:, halves[h]], sig[late][:, halves[h]], ALU.mult)
        nc.vector.tensor_reduce(low[:], z[:], mybir.AxisListType.X, ALU.max, negate=True)

        p = sb.tile([P, I], F32, name="p")
        total = sb.tile([P, 1], F32, name="total")
        nc.scalar.activation(p[:], z[:], ACT.Exp, bias=low[:], accum_out=total[:])
        inv = sb.tile([P, 1], F32, name="inv")
        factor = sb.tile([P, 1], F32, name="factor")
        ex = sb.tile([P, I], F32, name="ex")
        th = sb.tile([P, I], F32, name="th")
        res = sb.tile([P, I], F32, name="res")

        nc.vector.reciprocal(inv[:], total[:])
        nc.vector.tensor_scalar(ex[:], p[:], level_t[:], 0.0, ALU.subtract, ALU.max)
        nc.vector.tensor_scalar(factor[:], inv[:], gain_t[:], 128.0, ALU.mult, ALU.mult)
        quarter = I // 4
        for n in range(4):
            cols = slice(n * quarter, (n + 1) * quarter)
            nc.scalar.activation(th[:, cols], ex[:, cols], ACT.Tanh, scale=factor[:])
            nc.vector.tensor_tensor(res[:, cols], th[:, cols], base_t[:, cols], ALU.add)
        for cols, queue in (
            (slice(0, 2 * quarter), nc.sync),
            (slice(2 * quarter, 3 * quarter), nc.sync),
            (slice(3 * quarter, I), nc.scalar),
        ):
            queue.dma_start(out=out[:, cols], in_=res[:, cols])
